import numpy as np
import ml_dtypes

BF16 = ml_dtypes.bfloat16


def bf(x):
    return np.asarray(x, np.float32).astype(BF16)


def f32(x):
    return np.asarray(x, np.float32)


def f64(x):
    return np.asarray(x).astype(np.float64)


def striped(idx):
    return np.tile(idx.reshape(-1, 16).T, (8, 1))


S, K, M, N, E, Q = 256, 256, 128, 256, 4, 64


def setup_inputs():
    return {"base": bf(np.random.standard_normal((M, S))), "x": bf(np.random.standard_normal((K, N))), "w": bf(np.random.standard_normal((E, K, M)) / np.sqrt(K)), "s": f32(0.5 + np.random.random_sample((M, 1))), "b": f32(0.5 * np.random.standard_normal((M, 1))), "offs": striped(np.random.permutation(S))}


def reference(base, x, w, s, b, offs):
    idx = offs[:16].T.reshape(-1)
    z = f64(base).copy()
    for e in range(E):
        z[:, idx[e * Q : (e + 1) * Q]] += f64(w)[e].T @ f64(x)[:, e * Q : (e + 1) * Q]
    return z * f64(s) + f64(b)

@@ -1,0 +1,59 @@
+import concourse.mybir as mybir
+from concourse.masks import make_identity
+
+BF16, F32, U16 = mybir.dt.bfloat16, mybir.dt.float32, mybir.dt.uint16
+MULT, ADD = mybir.AluOpType.mult, mybir.AluOpType.add
+
+P = 128
+TOKENS = 256
+ENTRIES = 256
+EXPERTS = 4
+PIECE = ENTRIES // EXPERTS
+K_BLOCKS = 256 // P
+PIECE_COLUMNS = PIECE // 16
+
+FLOPS = 2 * 256 * P * ENTRIES
+
+
+def tile_scatter_matmul_kernel(tc, base, x, w, s, b, offs, out):
+    nc = tc.nc
+    with (
+        tc.tile_pool(name="held", bufs=1) as held,
+        tc.psum_pool(name="psum", bufs=1) as psum,
+    ):
+        offsets = held.tile([P, ENTRIES // 16], U16, name="offsets")
+        nc.sync.dma_start(offsets[:], offs)
+
+        ident = held.tile([P, P], BF16, name="ident")
+        make_identity(nc, ident[:])
+
+        base_tile = held.tile([P, TOKENS], BF16, name="base_tile")
+        nc.scalar.dma_start(base_tile[:], base)
+
+        x_tile = held.tile([P, K_BLOCKS, ENTRIES], BF16, name="x_tile")
+        nc.sync.dma_start(x_tile[:], x.rearrange("(kb p) j -> p kb j", p=P))
+        w_tile = held.tile([P, EXPERTS * K_BLOCKS, P], BF16, name="w_tile")
+        nc.gpsimd.dma_start(w_tile[:], w.rearrange("e (kb p) m -> p (e kb) m", p=P))
+
+        gain = held.tile([P, 1], F32, name="gain")
+        nc.scalar.dma_start(gain[:], s)
+        shift = held.tile([P, 1], F32, name="shift")
+        nc.scalar.dma_start(shift[:], b)
+
+        window = psum.tile([P, TOKENS], F32, name="window")
+        nc.tensor.matmul(window[:], ident[:], base_tile[:], start=True, stop=False)
+
+        for e in range(EXPERTS):
+            piece = offsets[:, e * PIECE_COLUMNS : (e + 1) * PIECE_COLUMNS]
+            for kb in range(K_BLOCKS):
+                nc.tensor.matmul(
+                    window[:].indirect(piece),
+                    w_tile[:, e * K_BLOCKS + kb, :],
+                    x_tile[:, kb, e * PIECE : (e + 1) * PIECE],
+                    start=False,
+                    stop=(e == EXPERTS - 1 and kb == K_BLOCKS - 1),
+                )
+
+        result = held.tile([P, TOKENS], F32, name="result")
+        nc.vector.tensor_scalar(result[:], window[:], gain[:], shift[:], MULT, ADD)
+        nc.sync.dma_start(out, result[:])

@@ -28,15 +28,20 @@ def tile_scatter_matmul_kernel(tc, base, x, w, s, b, offs, out):
         make_identity(nc, ident[:])
 
         base_tile = held.tile([P, TOKENS], BF16, name="base_tile")
-        nc.scalar.dma_start(base_tile[:], base)
+        nc.sync.dma_start(base_tile[:], base)
 
         x_tile = held.tile([P, K_BLOCKS, ENTRIES], BF16, name="x_tile")
-        nc.sync.dma_start(x_tile[:], x.rearrange("(kb p) j -> p kb j", p=P))
-        w_tile = held.tile([P, EXPERTS * K_BLOCKS, P], BF16, name="w_tile")
-        nc.gpsimd.dma_start(w_tile[:], w.rearrange("e (kb p) m -> p (e kb) m", p=P))
+        nc.scalar.dma_start(x_tile[:], x.rearrange("(kb p) j -> p kb j", p=P))
+
+        w_tiles = []
+        for e in range(EXPERTS):
+            w_tile = held.tile([P, K_BLOCKS, P], BF16, name="w_tile%d" % e)
+            queue = nc.sync if e % 2 == 0 else nc.scalar
+            queue.dma_start(w_tile[:], w[e].rearrange("(kb p) m -> p kb m", p=P))
+            w_tiles.append(w_tile)
 
         gain = held.tile([P, 1], F32, name="gain")
-        nc.scalar.dma_start(gain[:], s)
+        nc.sync.dma_start(gain[:], s)
         shift = held.tile([P, 1], F32, name="shift")
         nc.scalar.dma_start(shift[:], b)
 
@@ -48,7 +53,7 @@ def tile_scatter_matmul_kernel(tc, base, x, w, s, b, offs, out):
             for kb in range(K_BLOCKS):
                 nc.tensor.matmul(
                     window[:].indirect(piece),
-                    w_tile[:, e * K_BLOCKS + kb, :],
+                    w_tiles[e][:, kb, :],
                     x_tile[:, kb, e * PIECE : (e + 1) * PIECE],
                     start=False,
                     stop=(e == EXPERTS - 1 and kb == K_BLOCKS - 1),

@@ -31,13 +31,13 @@ def tile_scatter_matmul_kernel(tc, base, x, w, s, b, offs, out):
         nc.sync.dma_start(base_tile[:], base)
 
         x_tile = held.tile([P, K_BLOCKS, ENTRIES], BF16, name="x_tile")
-        nc.scalar.dma_start(x_tile[:], x.rearrange("(kb p) j -> p kb j", p=P))
+        nc.scalar.dma_start(x_tile[:], x.rearrange("(p kb) j -> p kb j", p=P))
 
         w_tiles = []
         for e in range(EXPERTS):
             w_tile = held.tile([P, K_BLOCKS, P], BF16, name="w_tile%d" % e)
             queue = nc.sync if e % 2 == 0 else nc.scalar
-            queue.dma_start(w_tile[:], w[e].rearrange("(kb p) m -> p kb m", p=P))
+            queue.dma_start(w_tile[:], w[e].rearrange("(p kb) m -> p kb m", p=P))
             w_tiles.append(w_tile)
 
         gain = held.tile([P, 1], F32, name="gain")

@@ -12,6 +12,9 @@ PIECE = ENTRIES // EXPERTS
 K_BLOCKS = 256 // P
 PIECE_COLUMNS = PIECE // 16
 
+WARM_MATMULS = 6
+WARM_COLUMNS = 256
+
 FLOPS = 2 * 256 * P * ENTRIES
 
 
@@ -21,6 +24,12 @@ def tile_scatter_matmul_kernel(tc, base, x, w, s, b, offs, out):
         tc.tile_pool(name="held", bufs=1) as held,
         tc.psum_pool(name="psum", bufs=1) as psum,
     ):
+        zeros = held.tile([P, WARM_COLUMNS], BF16, name="zeros")
+        nc.vector.memset(zeros[:], 0.0)
+        unread = psum.tile([P, WARM_COLUMNS], F32, name="unread")
+        for i in range(WARM_MATMULS):
+            nc.tensor.matmul(unread[:], zeros[:, :P], zeros[:], start=True, stop=True)
+
         offsets = held.tile([P, ENTRIES // 16], U16, name="offsets")
         nc.sync.dma_start(offsets[:], offs)
 
@@ -31,13 +40,13 @@ def tile_scatter_matmul_kernel(tc, base, x, w, s, b, offs, out):
         nc.sync.dma_start(base_tile[:], base)
 
         x_tile = held.tile([P, K_BLOCKS, ENTRIES], BF16, name="x_tile")
-        nc.scalar.dma_start(x_tile[:], x.rearrange("(p kb) j -> p kb j", p=P))
+        nc.scalar.dma_start(x_tile[:], x.rearrange("(kb p) j -> p kb j", p=P))
 
         w_tiles = []
         for e in range(EXPERTS):
             w_tile = held.tile([P, K_BLOCKS, P], BF16, name="w_tile%d" % e)
             queue = nc.sync if e % 2 == 0 else nc.scalar
-            queue.dma_start(w_tile[:], w[e].rearrange("(p kb) m -> p kb m", p=P))
+            queue.dma_start(w_tile[:], w[e].rearrange("(kb p) m -> p kb m", p=P))
             w_tiles.append(w_tile)
 
         gain = held.tile([P, 1], F32, name="gain")

@@ -37,16 +37,16 @@ def tile_scatter_matmul_kernel(tc, base, x, w, s, b, offs, out):
         make_identity(nc, ident[:])
 
         base_tile = held.tile([P, TOKENS], BF16, name="base_tile")
-        nc.sync.dma_start(base_tile[:], base)
+        nc.scalar.dma_start(base_tile[:], base)
 
         x_tile = held.tile([P, K_BLOCKS, ENTRIES], BF16, name="x_tile")
-        nc.scalar.dma_start(x_tile[:], x.rearrange("(kb p) j -> p kb j", p=P))
+        nc.sync.dma_start(x_tile[:], x.rearrange("(p kb) j -> p kb j", p=P))
 
         w_tiles = []
         for e in range(EXPERTS):
             w_tile = held.tile([P, K_BLOCKS, P], BF16, name="w_tile%d" % e)
-            queue = nc.sync if e % 2 == 0 else nc.scalar
-            queue.dma_start(w_tile[:], w[e].rearrange("(kb p) m -> p kb m", p=P))
+            queue = nc.scalar if e % 2 == 0 else nc.sync
+            queue.dma_start(w_tile[:], w[e].rearrange("(p kb) m -> p kb m", p=P))
             w_tiles.append(w_tile)
 
         gain = held.tile([P, 1], F32, name="gain")

@@ -37,7 +37,7 @@ def tile_scatter_matmul_kernel(tc, base, x, w, s, b, offs, out):
         make_identity(nc, ident[:])
 
         base_tile = held.tile([P, TOKENS], BF16, name="base_tile")
-        nc.scalar.dma_start(base_tile[:], base)
+        nc.sync.dma_start(base_tile[:], base)
 
         x_tile = held.tile([P, K_BLOCKS, ENTRIES], BF16, name="x_tile")
         nc.sync.dma_start(x_tile[:], x.rearrange("(p kb) j -> p kb j", p=P))
@@ -45,14 +45,13 @@ def tile_scatter_matmul_kernel(tc, base, x, w, s, b, offs, out):
         w_tiles = []
         for e in range(EXPERTS):
             w_tile = held.tile([P, K_BLOCKS, P], BF16, name="w_tile%d" % e)
-            queue = nc.scalar if e % 2 == 0 else nc.sync
-            queue.dma_start(w_tile[:], w[e].rearrange("(p kb) m -> p kb m", p=P))
+            nc.sync.dma_start(w_tile[:], w[e].rearrange("(p kb) m -> p kb m", p=P))
             w_tiles.append(w_tile)
 
         gain = held.tile([P, 1], F32, name="gain")
         nc.sync.dma_start(gain[:], s)
         shift = held.tile([P, 1], F32, name="shift")
-        nc.scalar.dma_start(shift[:], b)
+        nc.sync.dma_start(shift[:], b)
 
         window = psum.tile([P, TOKENS], F32, name="window")
         nc.tensor.matmul(window[:], ident[:], base_tile[:], start=True, stop=False)

@@ -37,7 +37,7 @@ def tile_scatter_matmul_kernel(tc, base, x, w, s, b, offs, out):
         make_identity(nc, ident[:])
 
         base_tile = held.tile([P, TOKENS], BF16, name="base_tile")
-        nc.sync.dma_start(base_tile[:], base)
+        nc.scalar.dma_start(base_tile[:], base)
 
         x_tile = held.tile([P, K_BLOCKS, ENTRIES], BF16, name="x_tile")
         nc.sync.dma_start(x_tile[:], x.rearrange("(p kb) j -> p kb j", p=P))
@@ -45,7 +45,8 @@ def tile_scatter_matmul_kernel(tc, base, x, w, s, b, offs, out):
         w_tiles = []
         for e in range(EXPERTS):
             w_tile = held.tile([P, K_BLOCKS, P], BF16, name="w_tile%d" % e)
-            nc.sync.dma_start(w_tile[:], w[e].rearrange("(p kb) m -> p kb m", p=P))
+            queue = nc.scalar if e == 0 else nc.sync
+            queue.dma_start(w_tile[:], w[e].rearrange("(p kb) m -> p kb m", p=P))
             w_tiles.append(w_tile)
 
         gain = held.tile([P, 1], F32, name="gain")

@@ -25,7 +25,7 @@ def tile_scatter_matmul_kernel(tc, base, x, w, s, b, offs, out):
         tc.psum_pool(name="psum", bufs=1) as psum,
     ):
         zeros = held.tile([P, WARM_COLUMNS], BF16, name="zeros")
-        nc.vector.memset(zeros[:], 0.0)
+        nc.gpsimd.memset(zeros[:], 0.0)
         unread = psum.tile([P, WARM_COLUMNS], F32, name="unread")
         for i in range(WARM_MATMULS):
             nc.tensor.matmul(unread[:], zeros[:, :P], zeros[:], start=True, stop=True)

import concourse.mybir as mybir
from concourse.masks import make_identity

BF16, F32, U16 = mybir.dt.bfloat16, mybir.dt.float32, mybir.dt.uint16
MULT, ADD = mybir.AluOpType.mult, mybir.AluOpType.add

P = 128
TOKENS = 256
ENTRIES = 256
EXPERTS = 4
PIECE = ENTRIES // EXPERTS
K_BLOCKS = 256 // P
PIECE_COLUMNS = PIECE // 16

WARM_MATMULS = 6
WARM_COLUMNS = 256

FLOPS = 2 * 256 * P * ENTRIES


def tile_scatter_matmul_kernel(tc, base, x, w, s, b, offs, out):
    nc = tc.nc
    with (
        tc.tile_pool(name="held", bufs=1) as held,
        tc.psum_pool(name="psum", bufs=1) as psum,
    ):
        zeros = held.tile([P, WARM_COLUMNS], BF16, name="zeros")
        nc.gpsimd.memset(zeros[:], 0.0)
        unread = psum.tile([P, WARM_COLUMNS], F32, name="unread")
        for i in range(WARM_MATMULS):
            nc.tensor.matmul(unread[:], zeros[:, :P], zeros[:], start=True, stop=True)

        offsets = held.tile([P, ENTRIES // 16], U16, name="offsets")
        nc.sync.dma_start(offsets[:], offs)

        ident = held.tile([P, P], BF16, name="ident")
        make_identity(nc, ident[:])

        base_tile = held.tile([P, TOKENS], BF16, name="base_tile")
        nc.scalar.dma_start(base_tile[:], base)

        x_tile = held.tile([P, K_BLOCKS, ENTRIES], BF16, name="x_tile")
        nc.sync.dma_start(x_tile[:], x.rearrange("(p kb) j -> p kb j", p=P))

        w_tiles = []
        for e in range(EXPERTS):
            w_tile = held.tile([P, K_BLOCKS, P], BF16, name="w_tile%d" % e)
            queue = nc.scalar if e == 0 else nc.sync
            queue.dma_start(w_tile[:], w[e].rearrange("(p kb) m -> p kb m", p=P))
            w_tiles.append(w_tile)

        gain = held.tile([P, 1], F32, name="gain")
        nc.sync.dma_start(gain[:], s)
        shift = held.tile([P, 1], F32, name="shift")
        nc.sync.dma_start(shift[:], b)

        window = psum.tile([P, TOKENS], F32, name="window")
        nc.tensor.matmul(window[:], ident[:], base_tile[:], start=True, stop=False)

        for e in range(EXPERTS):
            piece = offsets[:, e * PIECE_COLUMNS : (e + 1) * PIECE_COLUMNS]
            for kb in range(K_BLOCKS):
                nc.tensor.matmul(
                    window[:].indirect(piece),
                    w_tiles[e][:, kb, :],
                    x_tile[:, kb, e * PIECE : (e + 1) * PIECE],
                    start=False,
                    stop=(e == EXPERTS - 1 and kb == K_BLOCKS - 1),
                )

        result = held.tile([P, TOKENS], F32, name="result")
        nc.vector.tensor_scalar(result[:], window[:], gain[:], shift[:], MULT, ADD)
        nc.sync.dma_start(out, result[:])
